import numpy as np
import ml_dtypes


def mxq(x, axis, fmt="e4m3"):
    dtype, down = {"e4m3": (ml_dtypes.float8_e4m3fn, 7), "e5m2": (ml_dtypes.float8_e5m2, 14)}[fmt]
    v = np.moveaxis(np.asarray(x, np.float32).astype(ml_dtypes.bfloat16).astype(np.float64), axis, -1)
    blocks = v.reshape(v.shape[:-1] + (-1, 32))
    amax = np.abs(blocks).max(-1, keepdims=True)
    byte = np.maximum(np.where(amax > 0, np.frexp(amax)[1] - 1 + 127, 0) - down, 1)
    scale = np.exp2(byte - 127.0)
    codes = (blocks / scale).astype(np.float32).astype(dtype).astype(np.float64)
    return np.moveaxis((codes * scale).reshape(v.shape), -1, axis)


WIDE = False


def mx_kscale(k):
    if not WIDE:
        return np.ones(k)
    levels = np.array([10, -10, 5, -5, 0])
    if k % 512:
        return np.exp2(np.random.permutation(np.resize(levels, k // 32))).repeat(32)
    a = np.empty((k // 512, 16))
    for p in range(k // 512):
        a[p, :8] = np.random.permutation(np.resize(levels, 8))
        for g in range(8):
            far = levels[np.abs(levels - a[p, g]) >= 10]
            a[p, g + 8] = far[np.random.randint(len(far))]
    return np.exp2(a.ravel()).repeat(32)


def f64(x):
    return np.asarray(x).astype(np.float64)


def striped(idx):
    return np.tile(idx.reshape(-1, 16).T, (8, 1)).astype(np.uint16)


def unstriped(offs):
    return offs[:16].T.reshape(-1).astype(np.int64)


E2M1 = np.array([0.0, 0.5, 1.0, 1.5, 2.0, 3.0, 4.0, 6.0, -0.0, -0.5, -1.0, -1.5, -2.0, -3.0, -4.0, -6.0])


def pack_weight(w, fmt):
    k, n = w.shape
    w = f64(np.asarray(w, np.float32).astype(ml_dtypes.bfloat16)).reshape(k // 32, 32, n)
    amax = np.abs(w).max(1)
    if fmt == "e4m3":
        byte = np.frexp(amax)[1] - 1 + 127 - 7
    else:
        mant, ex = np.frexp(amax / 6.0)
        byte = np.where(mant > 0.5, ex, ex - 1) + 127
    byte = np.clip(np.where(amax > 0, byte, 1), 1, 254)
    scaled = (w * np.exp2(127.0 - byte)[:, None, :]).reshape(k, n).astype(np.float32)
    by_word = np.ascontiguousarray(scaled.reshape(k // 512, 128, 4, n).transpose(0, 1, 3, 2))
    if fmt == "e4m3":
        words = by_word.astype(ml_dtypes.float8_e4m3fn).view(np.uint8)
    else:
        c = by_word.astype(ml_dtypes.float4_e2m1fn).view(np.uint8) & 0xF
        words = (c[..., 0::2] | (c[..., 1::2] << 4)).reshape(k // 512, 128, 2 * n)
    return np.ascontiguousarray(words), np.ascontiguousarray(byte.astype(np.uint8).reshape(k // 512, 16, n))


def unpack_weight(words, scales, fmt):
    g, _, n = scales.shape
    words = np.ascontiguousarray(words).reshape(g, 128, n, -1)
    if fmt == "e4m3":
        vals = words.view(ml_dtypes.float8_e4m3fn).astype(np.float64)
    else:
        nib = np.empty((g, 128, n, 4), np.uint8)
        nib[..., 0::2] = words & 0xF
        nib[..., 1::2] = words >> 4
        vals = E2M1[nib]
    vals = vals * np.repeat(np.exp2(scales.astype(np.float64) - 127.0), 8, axis=1)[..., None]
    return vals.transpose(0, 1, 3, 2).reshape(g * 512, n)


def silu(v):
    return v / (1.0 + np.exp(-np.maximum(v, -700.0)))


K, T, E, C, H, N = 1024, 1024, 6, 128, 512, 512


def by_expert(wq, xq):
    return np.concatenate([wq[e].T @ xq[:, e * C:(e + 1) * C] for e in range(E)], axis=1)


def setup_inputs():
    n = np.random.standard_normal
    s = mx_kscale(K)
    u = mx_kscale(H)
    slot_token = np.random.permutation(T)[:E * C]
    partner = np.concatenate([np.random.permutation(T) for _ in range(-(-E * C // T))])[:E * C]
    x = pack_weight(n((K, T)) * s[:, None], "e4m3")
    w1 = [pack_weight(m, "e2m1") for m in n((E, K, H)) / np.sqrt(K) / s[None, :, None] * u]
    w2 = [pack_weight(m, "e2m1") for m in n((E, H, N)) / np.sqrt(H) / u[None, :, None]]
    return {
        "x_words": x[0],
        "x_scales": x[1],
        "w1_words": np.stack([m[0] for m in w1]),
        "w1_scales": np.stack([m[1] for m in w1]),
        "wp": (n((E, K, H)) / np.sqrt(K) / s[None, :, None] * u).astype(np.float32),
        "w2_words": np.stack([m[0] for m in w2]),
        "w2_scales": np.stack([m[1] for m in w2]),
        "gate": np.tile(np.random.uniform(0.2, 1.0, E * C), (128, 1)).astype(np.float32),
        "offs": striped(slot_token),
        "offs2": striped(partner),
    }


def reference(x_words, x_scales, w1_words, w1_scales, wp, w2_words, w2_scales, gate, offs, offs2):
    w1 = np.stack([unpack_weight(w1_words[e], w1_scales[e], "e2m1") for e in range(E)])
    wpq = mxq(f64(wp), 1, "e4m3")
    w2 = np.stack([unpack_weight(w2_words[e], w2_scales[e], "e2m1") for e in range(E)])
    idx, idx2 = unstriped(offs), unstriped(offs2)
    x = unpack_weight(x_words, x_scales, "e4m3")
    h = silu(by_expert(w1, x[:, idx]) + by_expert(wpq, x[:, idx2]))
    y = by_expert(w2, mxq(h, 0, "e4m3"))
    out = np.zeros((N, T))
    out[:, idx] = f64(gate[:1]) * y
    return out

@@ -1,0 +1,388 @@
+from contextlib import ExitStack
+
+import concourse.mybir as mybir
+from concourse.masks import make_identity
+
+K, T, E, C, H, N = 1024, 1024, 6, 128, 512, 512
+FLOPS = 2 * E * C * (2 * K * H + H * N)
+
+F32 = mybir.dt.float32
+BF16 = mybir.dt.bfloat16
+I32 = mybir.dt.int32
+U32 = mybir.dt.uint32
+U16 = mybir.dt.uint16
+U8 = mybir.dt.uint8
+FP8X4 = mybir.dt.float8_e4m3fn_x4
+FP4X4 = mybir.dt.float4_e2m1fn_x4
+SILU = mybir.ActivationFunctionType.Silu
+MULT = mybir.AluOpType.mult
+
+P = 128
+PACK = 4
+K_PASS = P * PACK
+PASSES = K // K_PASS
+SLOTS = E * C
+LIST_COL = 16
+GATHER_EXPERTS = 2
+N_TILES = N // P
+HALF = H // 2
+
+
+def tile_moe_duo_silu_kernel(
+    tc, x_words, x_scales, w1_words, w1_scales, wp, w2_words, w2_scales, gate, offs, offs2, out
+):
+    nc = tc.nc
+    with ExitStack() as ctx:
+        lists = ctx.enter_context(tc.tile_pool(name="lists", bufs=1))
+        keep = ctx.enter_context(tc.tile_pool(name="keep", bufs=1))
+        ring = ctx.enter_context(tc.tile_pool(name="ring", bufs=3))
+        arena = ctx.enter_context(tc.tile_pool(name="arena", bufs=1))
+        psum = ctx.enter_context(tc.psum_pool(name="psum", bufs=2))
+
+        def placed(shape, dtype, name, offset):
+            return arena.tile(shape, dtype, name=name, align_bytes=64, offset=offset)
+
+        def held(shape, dtype, name):
+            return keep.tile(shape, dtype, name=name, align_bytes=64)
+
+        token_list = lists.tile([P, SLOTS // LIST_COL], U16, name="token_list")
+        partner_list = lists.tile([P, SLOTS // LIST_COL], U16, name="partner_list")
+        index_lists = (token_list, partner_list)
+
+        xw = [held([P, T], U32, "xw%d" % s) for s in range(PASSES)]
+        xs = held([P, PASSES, T], U8, "xs")
+        w1s = held([P, E * PASSES, H], U8, "w1s")
+        w2s = held([P, E, N], U8, "w2s")
+        w1w = [held([P, PASSES, 2 * H], U8, "w1w%d" % e) for e in range(E)]
+        w2w = [held([P, 2 * N], U8, "w2w%d" % e) for e in range(E)]
+        wp_raw = {}
+        gate_sb = {}
+        result = [held([P, T], F32, "result%d" % c) for c in range(N_TILES)]
+        ident = held([P, P], F32, "ident")
+        zero_in = held([P, 1], F32, "zero_in")
+        zero_bias = held([P, 1], F32, "zero_bias")
+
+        def as_i32(plane):
+            return plane[:].rearrange("p a b -> p (a b)").bitcast(I32)
+
+        nc.vector.memset(as_i32(xs), 0)
+        nc.vector.memset(zero_in[:], 0.0)
+        nc.scalar.activation(out=zero_bias[:], in_=zero_in[:], func=SILU)
+        nc.vector.memset(as_i32(w1s), 0)
+        nc.vector.memset(result[0][:], 0.0)
+        nc.gpsimd.memset(as_i32(w2s), 0)
+        make_identity(nc, ident[:])
+        for c in range(1, N_TILES):
+            nc.gpsimd.memset(result[c][:], 0.0)
+
+        def load_scales(plane, rows):
+            for r in range(4):
+                nc.sync.dma_start(
+                    out=plane[r:P:32, :, :].bitcast(I32),
+                    in_=rows[:, r:16:4, :].rearrange("g q n -> q g n").bitcast(I32),
+                )
+
+        def load_x(s):
+            nc.sync.dma_start(out=xw[s][:].bitcast(I32), in_=x_words[s].rearrange("p t d -> p (t d)").bitcast(I32))
+
+        def load_wp(e, s, offset):
+            wp_raw[(e, s)] = placed([P, PACK, H], F32, "wp_raw%d_%d" % (e, s), offset)
+            rows = wp[e, s * K_PASS : (s + 1) * K_PASS, :].rearrange("(p j) i -> p j i", j=PACK)
+            nc.sync.dma_start(out=wp_raw[(e, s)][:], in_=rows)
+
+        def load_x_scales_both():
+            for q in range(4):
+                nc.sync.dma_start(
+                    out=xs[32 * q : 32 * q + 8, 0, :].bitcast(I32), in_=x_scales[:, 4 * q : 4 * q + 4, :].bitcast(I32)
+                )
+
+        def load_x_scales_second():
+            for r in range(4):
+                nc.sync.dma_start(out=xs[r:P:32, 1, :].bitcast(I32), in_=x_scales[1, r:16:4, :].bitcast(I32))
+
+        def load_gate(first, last):
+            part = held([P, (last - first) * C], F32, "gate%d" % first)
+            nc.sync.dma_start(out=part[:], in_=gate[:, first * C : last * C])
+            for e in range(first, last):
+                gate_sb[e] = part[:, (e - first) * C : (e - first + 1) * C]
+
+        def load_w1(e):
+            nc.sync.dma_start(out=w1w[e][:].bitcast(I32), in_=w1_words[e].rearrange("s p b -> p s b").bitcast(I32))
+
+        def load_w2(e):
+            nc.sync.dma_start(out=w2w[e][:].bitcast(I32), in_=w2_words[e, 0].bitcast(I32))
+
+        gathered_words = {}
+        gathered_scales = {}
+        n_group = GATHER_EXPERTS * C
+
+        def list_slice(group, which):
+            return index_lists[which][:, group * n_group // LIST_COL : (group + 1) * n_group // LIST_COL]
+
+        def gather_words(group, which, s, offset):
+            words = placed([P, n_group], U32, "gw%d_%d_%d" % (group, which, s), offset)
+            nc.vector.tensor_copy(out=words[:], in_=xw[s][:].indirect(list_slice(group, which)))
+            gathered_words[(group, which, s)] = words
+
+        def gather_scales(group, which, s, offset):
+            scales = placed([P, n_group], U8, "gs%d_%d_%d" % (group, which, s), offset)
+            nc.vector.tensor_copy(out=scales[:], in_=xs[:, s, :].indirect(list_slice(group, which)))
+            gathered_scales[(group, which, s)] = scales
+
+        grouped = {}
+        wp_q = {}
+
+        def new_grouped(e, s, offset):
+            grouped[(e, s)] = placed([P, PACK * H], BF16, "grouped%d_%d" % (e, s), offset)
+
+        def cast_wp(copy, e, s, first, last):
+            copy(
+                out=grouped[(e, s)][:, PACK * first : PACK * last].rearrange("p (c i t) -> p c t i", i=2, t=PACK),
+                in_=wp_raw[(e, s)][:, :, first:last].rearrange("p t (c i) -> p c t i", i=2),
+            )
+
+        def quantise_wp(e, s):
+            codes = ring.tile([P, H], U32, name="wp_codes", align_bytes=64, bufs=4)
+            scales = ring.tile([P, H], U8, name="wp_scales", align_bytes=64, bufs=4)
+            nc.vector.quantize_mx(out=codes[:].bitcast(FP8X4), scales=scales[:], in_=grouped[(e, s)][:])
+            wp_q[(e, s)] = (codes, scales)
+
+        pre = {}
+        turned = {}
+        h_grouped = {}
+        y = {}
+        y_sb = {}
+
+        def layer1(e, partner_passes):
+            group, place = divmod(e, GATHER_EXPERTS)
+            cols = slice(place * C, (place + 1) * C)
+            pre[e] = psum.tile([P, H], F32, name="pre", bufs=1)
+            for s in range(PASSES):
+                nc.tensor.matmul_mx(
+                    out=pre[e][:], lhsT=gathered_words[(group, 0, s)][:, cols].bitcast(FP8X4),
+                    lhsT_scale=gathered_scales[(group, 0, s)][:, cols],
+                    rhs=w1w[e][:, s, :].bitcast(FP4X4), rhs_scale=w1s[:, e * PASSES + s, :],
+                    start=(s == 0), stop=False,
+                )
+            for s in partner_passes:
+                codes, code_scales = wp_q[(e, s)]
+                nc.tensor.matmul_mx(
+                    out=pre[e][:], lhsT=gathered_words[(group, 1, s)][:, cols].bitcast(FP8X4),
+                    lhsT_scale=gathered_scales[(group, 1, 0)][4 * s : P, cols],
+                    rhs=codes[:].bitcast(FP8X4), rhs_scale=code_scales[:],
+                    start=False, stop=(s == partner_passes[-1]),
+                )
+
+        def activate(e, offset):
+            h = placed([P, H], BF16, "h%d" % e, offset)
+            nc.scalar.activation(
+                out=h[:].rearrange("c (u p d) -> c u p d", u=2, d=2),
+                in_=pre[e][:].rearrange("c (p u d) -> c u p d", u=2, d=2),
+                func=SILU, bias=zero_bias[:],
+            )
+            h_words = h[:].bitcast(F32)
+            turned[e] = psum.tile([P, 2, C], F32, name="turned")
+            for u in range(2):
+                nc.tensor.transpose(turned[e][:, u, :], h_words[:, u * P : (u + 1) * P], ident[:])
+
+        def regroup_h(e, offset):
+            h_grouped[e] = placed([P, PACK * C], BF16, "h_grouped%d" % e, offset)
+            nc.scalar.copy(
+                out=h_grouped[e][:].bitcast(F32).rearrange("p (c u) -> p c u", u=2),
+                in_=turned[e][:].rearrange("p u c -> p c u"),
+            )
+
+        def layer2(e):
+            codes = ring.tile([P, C], U32, name="h_codes", align_bytes=64)
+            scales = ring.tile([P, C], U8, name="h_scales", align_bytes=64)
+            nc.vector.quantize_mx(out=codes[:].bitcast(FP8X4), scales=scales[:], in_=h_grouped[e][:])
+            y[e] = psum.tile([P, N_TILES, C], F32, name="y", bufs=3)
+            for c in range(N_TILES):
+                nc.tensor.matmul_mx(
+                    out=y[e][:, c, :], lhsT=w2w[e][:, 2 * P * c : 2 * P * (c + 1)].bitcast(FP4X4),
+                    lhsT_scale=w2s[:, e, P * c : P * (c + 1)],
+                    rhs=codes[:].bitcast(FP8X4), rhs_scale=scales[:], start=True, stop=True,
+                )
+
+        def drain_y(e, half, offset):
+            y_sb[(e, half)] = placed([P, 2, C], F32, "y_sb%d_%d" % (e, half), offset)
+            nc.scalar.copy(out=y_sb[(e, half)][:], in_=y[e][:, 2 * half : 2 * half + 2, :])
+
+        def scatter(e, c):
+            cols = slice(e * C // LIST_COL, (e + 1) * C // LIST_COL)
+            nc.vector.tensor_tensor(result[c][:].indirect(token_list[:, cols]), y_sb[(e, c // 2)][:, c % 2, :], gate_sb[e], MULT)
+
+        def store(c):
+            nc.sync.dma_start(out=out[c * P : (c + 1) * P, :], in_=result[c][:])
+
+        load_w1(0)
+        nc.sync.dma_start(token_list[:], offs)
+        load_x_scales_both()
+        load_wp(0, 0, 0)
+        load_x(1)
+        nc.sync.dma_start(partner_list[:], offs2)
+        load_scales(w1s, w1_scales.rearrange("e s b i -> (e s) b i"))
+        load_x(0)
+        load_w1(1)
+        load_x_scales_second()
+        load_wp(0, 1, 8192)
+        load_wp(1, 0, 16384)
+        load_wp(1, 1, 24576)
+        load_wp(2, 0, 32768)
+        load_scales(w2s, w2_scales.rearrange("e s b n -> (e s) b n"))
+        load_gate(0, 4)
+        load_w2(0)
+        load_wp(2, 1, 40960)
+        load_w1(2)
+        load_wp(3, 0, 49152)
+        load_w2(1)
+        load_wp(3, 1, 57344)
+        load_w1(3)
+        load_wp(4, 0, 65536)
+        load_w2(2)
+        load_wp(4, 1, 73728)
+        load_w2(3)
+        load_w1(4)
+        load_wp(5, 0, 81920)
+        load_wp(5, 1, 90112)
+        load_w1(5)
+        load_w2(4)
+        load_gate(4, 6)
+        load_w2(5)
+        gather_words(0, 1, 1, 147456)
+        gather_words(2, 0, 0, 148480)
+        gather_words(0, 0, 1, 149504)
+        gather_words(0, 0, 0, 150528)
+        gather_scales(0, 0, 0, 151552)
+        gather_words(0, 1, 0, 151808)
+        gather_scales(0, 0, 1, 152832)
+        gather_scales(0, 1, 0, 153088)
+        gather_words(2, 1, 0, 153344)
+        gather_words(1, 0, 1, 154368)
+        gather_scales(2, 0, 0, 155392)
+        new_grouped(0, 0, 98304)
+        cast_wp(nc.scalar.copy, 0, 0, 0, 256)
+        cast_wp(nc.scalar.copy, 0, 0, 256, 512)
+        quantise_wp(0, 0)
+        gather_scales(2, 1, 0, 98368)
+        gather_words(2, 1, 1, 98624)
+        new_grouped(0, 1, 122880)
+        cast_wp(nc.scalar.copy, 0, 1, 0, 256)
+        cast_wp(nc.scalar.copy, 0, 1, 256, 512)
+        quantise_wp(0, 1)
+        gather_scales(1, 0, 1, 122944)
+        gather_words(1, 1, 0, 123200)
+        gather_words(1, 0, 0, 124224)
+        new_grouped(1, 0, 102336)
+        cast_wp(nc.scalar.copy, 1, 0, 0, 224)
+        cast_wp(nc.scalar.copy, 1, 0, 224, 448)
+        cast_wp(nc.vector.tensor_copy, 1, 0, 448, 512)
+        quantise_wp(1, 0)
+        gather_scales(1, 0, 0, 102400)
+        gather_words(2, 0, 1, 102656)
+        new_grouped(1, 1, 126912)
+        cast_wp(nc.scalar.copy, 1, 1, 0, 256)
+        layer1(0, (1, 0))
+        activate(0, 16384)
+        cast_wp(nc.scalar.copy, 1, 1, 256, 512)
+        quantise_wp(1, 1)
+        gather_scales(1, 1, 0, 126976)
+        gather_words(1, 1, 1, 127232)
+        gather_scales(2, 0, 1, 128256)
+        regroup_h(0, 17408)
+        layer2(0)
+        new_grouped(2, 0, 106368)
+        cast_wp(nc.scalar.copy, 2, 0, 0, 256)
+        cast_wp(nc.scalar.copy, 2, 0, 256, 512)
+        quantise_wp(2, 0)
+        layer1(1, (0, 1))
+        activate(1, 32768)
+        drain_y(0, 1, 0)
+        regroup_h(1, 18432)
+        layer2(1)
+        new_grouped(2, 1, 130944)
+        cast_wp(nc.scalar.copy, 2, 1, 0, 256)
+        drain_y(0, 0, 1024)
+        cast_wp(nc.scalar.copy, 2, 1, 256, 512)
+        quantise_wp(2, 1)
+        new_grouped(3, 0, 110400)
+        cast_wp(nc.scalar.copy, 3, 0, 0, 256)
+        drain_y(1, 1, 19456)
+        cast_wp(nc.scalar.copy, 3, 0, 256, 512)
+        quantise_wp(3, 0)
+        layer1(2, (0, 1))
+        activate(2, 33792)
+        regroup_h(2, 49152)
+        layer2(2)
+        new_grouped(3, 1, 134976)
+        cast_wp(nc.scalar.copy, 3, 1, 0, 192)
+        cast_wp(nc.scalar.copy, 3, 1, 192, 384)
+        cast_wp(nc.vector.tensor_copy, 3, 1, 384, 512)
+        quantise_wp(3, 1)
+        drain_y(1, 0, 20480)
+        new_grouped(4, 0, 114432)
+        cast_wp(nc.scalar.copy, 4, 0, 0, 224)
+        cast_wp(nc.scalar.copy, 4, 0, 224, 448)
+        cast_wp(nc.vector.tensor_copy, 4, 0, 448, 512)
+        quantise_wp(4, 0)
+        layer1(3, (0, 1))
+        activate(3, 50176)
+        drain_y(2, 0, 34816)
+        regroup_h(3, 51200)
+        layer2(3)
+        drain_y(2, 1, 50176)
+        new_grouped(4, 1, 139008)
+        cast_wp(nc.scalar.copy, 4, 1, 0, 256)
+        cast_wp(nc.scalar.copy, 4, 1, 256, 512)
+        quantise_wp(4, 1)
+        new_grouped(5, 0, 118464)
+        cast_wp(nc.scalar.copy, 5, 0, 0, 256)
+        cast_wp(nc.scalar.copy, 5, 0, 256, 512)
+        quantise_wp(5, 0)
+        drain_y(3, 0, 73728)
+        layer1(4, (0, 1))
+        activate(4, 65536)
+        new_grouped(5, 1, 143040)
+        cast_wp(nc.scalar.copy, 5, 1, 0, 160)
+        regroup_h(4, 66560)
+        layer2(4)
+        cast_wp(nc.scalar.copy, 5, 1, 160, 320)
+        cast_wp(nc.vector.tensor_copy, 5, 1, 320, 512)
+        quantise_wp(5, 1)
+        drain_y(4, 0, 67584)
+        layer1(5, (0, 1))
+        activate(5, 81920)
+        regroup_h(5, 82944)
+        layer2(5)
+        drain_y(5, 0, 83968)
+        drain_y(3, 1, 52224)
+        drain_y(5, 1, 84992)
+        drain_y(4, 1, 81920)
+        scatter(0, 0)
+        scatter(0, 1)
+        scatter(0, 2)
+        scatter(0, 3)
+        scatter(1, 0)
+        scatter(1, 1)
+        scatter(1, 2)
+        scatter(1, 3)
+        scatter(2, 0)
+        scatter(2, 1)
+        scatter(2, 2)
+        scatter(2, 3)
+        scatter(3, 0)
+        scatter(3, 1)
+        scatter(3, 2)
+        scatter(3, 3)
+        scatter(4, 3)
+        scatter(4, 1)
+        scatter(4, 2)
+        scatter(5, 2)
+        scatter(4, 0)
+        scatter(5, 0)
+        scatter(5, 3)
+        scatter(5, 1)
+        store(2)
+        store(0)
+        store(3)
+        store(1)

@@ -23,7 +23,7 @@ K_PASS = P * PACK
 PASSES = K // K_PASS
 SLOTS = E * C
 LIST_COL = 16
-GATHER_EXPERTS = 2
+GROUPS = ((0, 2), (2, 6))
 N_TILES = N // P
 HALF = H // 2
 
@@ -50,7 +50,8 @@ def tile_moe_duo_silu_kernel(
         index_lists = (token_list, partner_list)
 
         xw = [held([P, T], U32, "xw%d" % s) for s in range(PASSES)]
-        xs = held([P, PASSES, T], U8, "xs")
+        xs = held([P, T], U8, "xs")
+        token_scales_second = held([P, SLOTS], U8, "token_scales_second")
         w1s = held([P, E * PASSES, H], U8, "w1s")
         w2s = held([P, E, N], U8, "w2s")
         w1w = [held([P, PASSES, 2 * H], U8, "w1w%d" % e) for e in range(E)]
@@ -65,10 +66,11 @@ def tile_moe_duo_silu_kernel(
         def as_i32(plane):
             return plane[:].rearrange("p a b -> p (a b)").bitcast(I32)
 
-        nc.vector.memset(as_i32(xs), 0)
+        nc.vector.memset(xs[:].bitcast(I32), 0)
         nc.vector.memset(zero_in[:], 0.0)
         nc.scalar.activation(out=zero_bias[:], in_=zero_in[:], func=SILU)
         nc.vector.memset(as_i32(w1s), 0)
+        nc.vector.memset(token_scales_second[:].bitcast(I32), 0)
         nc.vector.memset(result[0][:], 0.0)
         nc.gpsimd.memset(as_i32(w2s), 0)
         make_identity(nc, ident[:])
@@ -93,12 +95,8 @@ def tile_moe_duo_silu_kernel(
         def load_x_scales_both():
             for q in range(4):
                 nc.sync.dma_start(
-                    out=xs[32 * q : 32 * q + 8, 0, :].bitcast(I32), in_=x_scales[:, 4 * q : 4 * q + 4, :].bitcast(I32)
+                    out=xs[32 * q : 32 * q + 8, :].bitcast(I32), in_=x_scales[:, 4 * q : 4 * q + 4, :].bitcast(I32)
                 )
-
-        def load_x_scales_second():
-            for r in range(4):
-                nc.sync.dma_start(out=xs[r:P:32, 1, :].bitcast(I32), in_=x_scales[1, r:16:4, :].bitcast(I32))
 
         def load_gate(first, last):
             part = held([P, (last - first) * C], F32, "gate%d" % first)
@@ -114,20 +112,24 @@ def tile_moe_duo_silu_kernel(
 
         gathered_words = {}
         gathered_scales = {}
-        n_group = GATHER_EXPERTS * C
-
-        def list_slice(group, which):
-            return index_lists[which][:, group * n_group // LIST_COL : (group + 1) * n_group // LIST_COL]
 
         def gather_words(group, which, s, offset):
-            words = placed([P, n_group], U32, "gw%d_%d_%d" % (group, which, s), offset)
-            nc.vector.tensor_copy(out=words[:], in_=xw[s][:].indirect(list_slice(group, which)))
-            gathered_words[(group, which, s)] = words
+            first, last = GROUPS[group]
+            words = placed([P, (last - first) * C], U32, "gw%d_%d_%d" % (group, which, s), offset)
+            cols = slice(first * C // LIST_COL, last * C // LIST_COL)
+            nc.vector.tensor_copy(out=words[:], in_=xw[s][:].indirect(index_lists[which][:, cols]))
+            for e in range(first, last):
+                gathered_words[(e, which, s)] = words[:, (e - first) * C : (e - first + 1) * C]
 
-        def gather_scales(group, which, s, offset):
-            scales = placed([P, n_group], U8, "gs%d_%d_%d" % (group, which, s), offset)
-            nc.vector.tensor_copy(out=scales[:], in_=xs[:, s, :].indirect(list_slice(group, which)))
-            gathered_scales[(group, which, s)] = scales
+        def gather_scales(which):
+            scales = held([P, SLOTS], U8, "gs%d" % which)
+            nc.vector.tensor_copy(out=scales[:], in_=xs[:].indirect(index_lists[which][:]))
+            gathered_scales[which] = scales
+            if which == 0:
+                for r in range(4):
+                    nc.sync.dma_start(
+                        out=token_scales_second[r:P:32, :].bitcast(I32), in_=scales[r + 4 : P : 32, :].bitcast(I32)
+                    )
 
         grouped = {}
         wp_q = {}
@@ -137,15 +139,18 @@ def tile_moe_duo_silu_kernel(
 
         def cast_wp(copy, e, s, first, last):
             copy(
-                out=grouped[(e, s)][:, PACK * first : PACK * last].rearrange("p (c i t) -> p c t i", i=2, t=PACK),
-                in_=wp_raw[(e, s)][:, :, first:last].rearrange("p t (c i) -> p c t i", i=2),
+                out=grouped[(e, s)][:, PACK * first : PACK * last].rearrange("p (c i t) -> p c t i", i=4, t=PACK),
+                in_=wp_raw[(e, s)][:, :, first:last].rearrange("p t (c i) -> p c t i", i=4),
             )
 
-        def quantise_wp(e, s):
-            codes = ring.tile([P, H], U32, name="wp_codes", align_bytes=64, bufs=4)
+        def quantise_wp(e, s, offset):
+            if offset is None:
+                codes = ring.tile([P, H], U32, name="wp_codes", align_bytes=64, bufs=4)
+            else:
+                codes = placed([P, H], U32, "wp_codes%d_%d" % (e, s), offset)
             scales = ring.tile([P, H], U8, name="wp_scales", align_bytes=64, bufs=4)
             nc.vector.quantize_mx(out=codes[:].bitcast(FP8X4), scales=scales[:], in_=grouped[(e, s)][:])
-            wp_q[(e, s)] = (codes, scales)
+            wp_q[(e, s)] = (codes[:].bitcast(FP8X4), scales[:])
 
         pre = {}
         turned = {}
@@ -153,24 +158,20 @@ def tile_moe_duo_silu_kernel(
         y = {}
         y_sb = {}
 
-        def layer1(e, partner_passes):
-            group, place = divmod(e, GATHER_EXPERTS)
-            cols = slice(place * C, (place + 1) * C)
+        def layer1(e, order):
+            cols = slice(e * C, (e + 1) * C)
+            token_scales = (gathered_scales[0], token_scales_second)
             pre[e] = psum.tile([P, H], F32, name="pre", bufs=1)
-            for s in range(PASSES):
+            for place, (which, s) in enumerate(order):
+                if which == 0:
+                    slot_scales = token_scales[s][:, cols]
+                    codes, code_scales = w1w[e][:, s, :].bitcast(FP4X4), w1s[:, e * PASSES + s, :]
+                else:
+                    slot_scales = gathered_scales[1][4 * s : P, cols]
+                    codes, code_scales = wp_q[(e, s)]
                 nc.tensor.matmul_mx(
-                    out=pre[e][:], lhsT=gathered_words[(group, 0, s)][:, cols].bitcast(FP8X4),
-                    lhsT_scale=gathered_scales[(group, 0, s)][:, cols],
-                    rhs=w1w[e][:, s, :].bitcast(FP4X4), rhs_scale=w1s[:, e * PASSES + s, :],
-                    start=(s == 0), stop=False,
-                )
-            for s in partner_passes:
-                codes, code_scales = wp_q[(e, s)]
-                nc.tensor.matmul_mx(
-                    out=pre[e][:], lhsT=gathered_words[(group, 1, s)][:, cols].bitcast(FP8X4),
-                    lhsT_scale=gathered_scales[(group, 1, 0)][4 * s : P, cols],
-                    rhs=codes[:].bitcast(FP8X4), rhs_scale=code_scales[:],
-                    start=False, stop=(s == partner_passes[-1]),
+                    out=pre[e][:], lhsT=gathered_words[(e, which, s)].bitcast(FP8X4), lhsT_scale=slot_scales,
+                    rhs=codes, rhs_scale=code_scales, start=(place == 0), stop=(place == len(order) - 1),
                 )
 
         def activate(e, offset):
@@ -204,160 +205,141 @@ def tile_moe_duo_silu_kernel(
                     rhs=codes[:].bitcast(FP8X4), rhs_scale=scales[:], start=True, stop=True,
                 )
 
-        def drain_y(e, half, offset):
-            y_sb[(e, half)] = placed([P, 2, C], F32, "y_sb%d_%d" % (e, half), offset)
-            nc.scalar.copy(out=y_sb[(e, half)][:], in_=y[e][:, 2 * half : 2 * half + 2, :])
+        def drain_y(e, first, last, offset):
+            part = placed([P, last - first, C], F32, "y_sb%d_%d" % (e, first), offset)
+            nc.scalar.copy(out=part[:], in_=y[e][:, first:last, :])
+            for c in range(first, last):
+                y_sb[(e, c)] = part[:, c - first, :]
 
         def scatter(e, c):
             cols = slice(e * C // LIST_COL, (e + 1) * C // LIST_COL)
-            nc.vector.tensor_tensor(result[c][:].indirect(token_list[:, cols]), y_sb[(e, c // 2)][:, c % 2, :], gate_sb[e], MULT)
+            nc.vector.tensor_tensor(result[c][:].indirect(token_list[:, cols]), y_sb[(e, c)], gate_sb[e], MULT)
 
         def store(c):
             nc.sync.dma_start(out=out[c * P : (c + 1) * P, :], in_=result[c][:])
 
-        load_w1(0)
-        nc.sync.dma_start(token_list[:], offs)
         load_x_scales_both()
-        load_wp(0, 0, 0)
+        nc.sync.dma_start(token_list[:], offs)
         load_x(1)
         nc.sync.dma_start(partner_list[:], offs2)
-        load_scales(w1s, w1_scales.rearrange("e s b i -> (e s) b i"))
-        load_x(0)
-        load_w1(1)
-        load_x_scales_second()
+        load_wp(0, 0, 0)
         load_wp(0, 1, 8192)
+        load_x(0)
+        load_scales(w1s, w1_scales.rearrange("e s b i -> (e s) b i"))
+        load_w1(0)
         load_wp(1, 0, 16384)
+        gather_scales(0)
         load_wp(1, 1, 24576)
+        load_w2(0)
         load_wp(2, 0, 32768)
         load_scales(w2s, w2_scales.rearrange("e s b n -> (e s) b n"))
-        load_gate(0, 4)
-        load_w2(0)
+        load_w1(1)
+        load_gate(0, 2)
         load_wp(2, 1, 40960)
-        load_w1(2)
         load_wp(3, 0, 49152)
+        load_w2(4)
         load_w2(1)
         load_wp(3, 1, 57344)
-        load_w1(3)
+        load_w1(2)
         load_wp(4, 0, 65536)
-        load_w2(2)
         load_wp(4, 1, 73728)
-        load_w2(3)
+        load_w1(3)
+        load_gate(2, 4)
+        load_w2(2)
         load_w1(4)
         load_wp(5, 0, 81920)
         load_wp(5, 1, 90112)
-        load_w1(5)
-        load_w2(4)
         load_gate(4, 6)
+        load_w2(3)
+        load_w1(5)
         load_w2(5)
-        gather_words(0, 1, 1, 147456)
-        gather_words(2, 0, 0, 148480)
-        gather_words(0, 0, 1, 149504)
-        gather_words(0, 0, 0, 150528)
-        gather_scales(0, 0, 0, 151552)
-        gather_words(0, 1, 0, 151808)
-        gather_scales(0, 0, 1, 152832)
-        gather_scales(0, 1, 0, 153088)
-        gather_words(2, 1, 0, 153344)
-        gather_words(1, 0, 1, 154368)
-        gather_scales(2, 0, 0, 155392)
+        gather_words(0, 1, 0, 147456)
+        gather_words(1, 1, 1, 148480)
+        gather_words(0, 0, 1, 150528)
+        gather_words(0, 0, 0, 151552)
+        gather_scales(1)
+        gather_words(0, 1, 1, 152576)
         new_grouped(0, 0, 98304)
-        cast_wp(nc.scalar.copy, 0, 0, 0, 256)
-        cast_wp(nc.scalar.copy, 0, 0, 256, 512)
-        quantise_wp(0, 0)
-        gather_scales(2, 1, 0, 98368)
-        gather_words(2, 1, 1, 98624)
+        cast_wp(nc.scalar.copy, 0, 0, 0, 512)
+        quantise_wp(0, 0, None)
         new_grouped(0, 1, 122880)
         cast_wp(nc.scalar.copy, 0, 1, 0, 256)
         cast_wp(nc.scalar.copy, 0, 1, 256, 512)
-        quantise_wp(0, 1)
-        gather_scales(1, 0, 1, 122944)
-        gather_words(1, 1, 0, 123200)
-        gather_words(1, 0, 0, 124224)
-        new_grouped(1, 0, 102336)
-        cast_wp(nc.scalar.copy, 1, 0, 0, 224)
-        cast_wp(nc.scalar.copy, 1, 0, 224, 448)
-        cast_wp(nc.vector.tensor_copy, 1, 0, 448, 512)
-        quantise_wp(1, 0)
-        gather_scales(1, 0, 0, 102400)
-        gather_words(2, 0, 1, 102656)
-        new_grouped(1, 1, 126912)
+        quantise_wp(0, 1, None)
+        gather_words(1, 0, 1, 122880)
+        gather_words(1, 0, 0, 124928)
+        new_grouped(1, 0, 102400)
+        cast_wp(nc.scalar.copy, 1, 0, 0, 512)
+        quantise_wp(1, 0, None)
+        new_grouped(1, 1, 126976)
         cast_wp(nc.scalar.copy, 1, 1, 0, 256)
-        layer1(0, (1, 0))
-        activate(0, 16384)
-        cast_wp(nc.scalar.copy, 1, 1, 256, 512)
-        quantise_wp(1, 1)
-        gather_scales(1, 1, 0, 126976)
-        gather_words(1, 1, 1, 127232)
-        gather_scales(2, 0, 1, 128256)
-        regroup_h(0, 17408)
-        layer2(0)
-        new_grouped(2, 0, 106368)
-        cast_wp(nc.scalar.copy, 2, 0, 0, 256)
-        cast_wp(nc.scalar.copy, 2, 0, 256, 512)
-        quantise_wp(2, 0)
-        layer1(1, (0, 1))
-        activate(1, 32768)
-        drain_y(0, 1, 0)
-        regroup_h(1, 18432)
-        layer2(1)
-        new_grouped(2, 1, 130944)
+        cast_wp(nc.vector.tensor_copy, 1, 1, 256, 512)
+        quantise_wp(1, 1, None)
+        gather_words(1, 1, 0, 126976)
+        new_grouped(2, 0, 106432)
+        cast_wp(nc.scalar.copy, 2, 0, 0, 512)
+        quantise_wp(2, 0, None)
+        layer1(0, ((1, 0), (0, 0), (0, 1), (1, 1)))
+        activate(0, 0)
+        layer1(1, ((1, 0), (0, 0), (0, 1), (1, 1)))
+        activate(1, 16384)
+        new_grouped(2, 1, 131008)
         cast_wp(nc.scalar.copy, 2, 1, 0, 256)
-        drain_y(0, 0, 1024)
+        regroup_h(1, 17408)
+        layer2(1)
         cast_wp(nc.scalar.copy, 2, 1, 256, 512)
-        quantise_wp(2, 1)
-        new_grouped(3, 0, 110400)
-        cast_wp(nc.scalar.copy, 3, 0, 0, 256)
-        drain_y(1, 1, 19456)
-        cast_wp(nc.scalar.copy, 3, 0, 256, 512)
-        quantise_wp(3, 0)
-        layer1(2, (0, 1))
-        activate(2, 33792)
-        regroup_h(2, 49152)
+        quantise_wp(2, 1, None)
+        new_grouped(3, 0, 110464)
+        cast_wp(nc.scalar.copy, 3, 0, 0, 192)
+        cast_wp(nc.vector.tensor_copy, 3, 0, 192, 512)
+        quantise_wp(3, 0, None)
+        regroup_h(0, 18432)
+        layer2(0)
+        drain_y(0, 0, 4, 19456)
+        new_grouped(3, 1, 135040)
+        cast_wp(nc.scalar.copy, 3, 1, 0, 512)
+        quantise_wp(3, 1, None)
+        layer1(2, ((1, 0), (0, 0), (0, 1), (1, 1)))
+        activate(2, 32768)
+        regroup_h(2, 57344)
         layer2(2)
-        new_grouped(3, 1, 134976)
-        cast_wp(nc.scalar.copy, 3, 1, 0, 192)
-        cast_wp(nc.scalar.copy, 3, 1, 192, 384)
-        cast_wp(nc.vector.tensor_copy, 3, 1, 384, 512)
-        quantise_wp(3, 1)
-        drain_y(1, 0, 20480)
-        new_grouped(4, 0, 114432)
-        cast_wp(nc.scalar.copy, 4, 0, 0, 224)
-        cast_wp(nc.scalar.copy, 4, 0, 224, 448)
-        cast_wp(nc.vector.tensor_copy, 4, 0, 448, 512)
-        quantise_wp(4, 0)
-        layer1(3, (0, 1))
-        activate(3, 50176)
-        drain_y(2, 0, 34816)
-        regroup_h(3, 51200)
+        new_grouped(4, 0, 114496)
+        cast_wp(nc.scalar.copy, 4, 0, 0, 384)
+        cast_wp(nc.vector.tensor_copy, 4, 0, 384, 512)
+        quantise_wp(4, 0, None)
+        drain_y(2, 2, 4, 33792)
+        layer1(3, ((1, 0), (1, 1), (0, 0), (0, 1)))
+        activate(3, 65536)
+        drain_y(1, 0, 2, 21504)
+        drain_y(1, 2, 4, 22528)
+        new_grouped(4, 1, 139072)
+        cast_wp(nc.scalar.copy, 4, 1, 0, 192)
+        cast_wp(nc.vector.tensor_copy, 4, 1, 192, 512)
+        quantise_wp(4, 1, None)
+        regroup_h(3, 73728)
         layer2(3)
-        drain_y(2, 1, 50176)
-        new_grouped(4, 1, 139008)
-        cast_wp(nc.scalar.copy, 4, 1, 0, 256)
-        cast_wp(nc.scalar.copy, 4, 1, 256, 512)
-        quantise_wp(4, 1)
-        new_grouped(5, 0, 118464)
-        cast_wp(nc.scalar.copy, 5, 0, 0, 256)
-        cast_wp(nc.scalar.copy, 5, 0, 256, 512)
-        quantise_wp(5, 0)
-        drain_y(3, 0, 73728)
-        layer1(4, (0, 1))
-        activate(4, 65536)
-        new_grouped(5, 1, 143040)
-        cast_wp(nc.scalar.copy, 5, 1, 0, 160)
+        new_grouped(5, 0, 118528)
+        cast_wp(nc.scalar.copy, 5, 0, 0, 512)
+        quantise_wp(5, 0, None)
+        layer1(4, ((1, 0), (0, 0), (0, 1), (1, 1)))
+        activate(4, 81920)
+        drain_y(2, 0, 2, 74752)
         regroup_h(4, 66560)
         layer2(4)
-        cast_wp(nc.scalar.copy, 5, 1, 160, 320)
-        cast_wp(nc.vector.tensor_copy, 5, 1, 320, 512)
-        quantise_wp(5, 1)
-        drain_y(4, 0, 67584)
-        layer1(5, (0, 1))
-        activate(5, 81920)
-        regroup_h(5, 82944)
+        new_grouped(5, 1, 143104)
+        cast_wp(nc.scalar.copy, 5, 1, 0, 256)
+        cast_wp(nc.vector.tensor_copy, 5, 1, 256, 512)
+        quantise_wp(5, 1, None)
+        layer1(5, ((0, 0), (0, 1), (1, 0), (1, 1)))
+        activate(5, 82944)
+        drain_y(3, 0, 2, 83968)
+        regroup_h(5, 84992)
         layer2(5)
-        drain_y(5, 0, 83968)
-        drain_y(3, 1, 52224)
-        drain_y(5, 1, 84992)
-        drain_y(4, 1, 81920)
+        drain_y(4, 2, 4, 82944)
+        drain_y(5, 0, 2, 86016)
+        drain_y(3, 2, 4, 81920)
+        drain_y(5, 2, 4, 87040)
+        drain_y(4, 0, 2, 90112)
         scatter(0, 0)
         scatter(0, 1)
         scatter(0, 2)
@@ -374,15 +356,15 @@ def tile_moe_duo_silu_kernel(
         scatter(3, 1)
         scatter(3, 2)
         scatter(3, 3)
-        scatter(4, 3)
         scatter(4, 1)
+        scatter(4, 0)
+        scatter(5, 1)
+        scatter(4, 3)
+        scatter(5, 3)
+        scatter(5, 0)
         scatter(4, 2)
         scatter(5, 2)
-        scatter(4, 0)
-        scatter(5, 0)
-        scatter(5, 3)
-        scatter(5, 1)
-        store(2)
-        store(0)
-        store(3)
         store(1)
+        store(3)
+        store(0)
+        store(2)

@@ -207,139 +207,141 @@ def tile_moe_duo_silu_kernel(
 
         def drain_y(e, first, last, offset):
             part = placed([P, last - first, C], F32, "y_sb%d_%d" % (e, first), offset)
-            nc.scalar.copy(out=part[:], in_=y[e][:, first:last, :])
+            weights = gate_sb[e].unsqueeze(1).to_broadcast([P, last - first, C])
+            nc.vector.tensor_tensor(part[:], y[e][:, first:last, :], weights, MULT)
             for c in range(first, last):
                 y_sb[(e, c)] = part[:, c - first, :]
 
         def scatter(e, c):
             cols = slice(e * C // LIST_COL, (e + 1) * C // LIST_COL)
-            nc.vector.tensor_tensor(result[c][:].indirect(token_list[:, cols]), y_sb[(e, c)], gate_sb[e], MULT)
+            nc.vector.tensor_copy(out=result[c][:].indirect(token_list[:, cols]), in_=y_sb[(e, c)])
 
         def store(c):
             nc.sync.dma_start(out=out[c * P : (c + 1) * P, :], in_=result[c][:])
 
-        load_x_scales_both()
-        nc.sync.dma_start(token_list[:], offs)
-        load_x(1)
+        load_x(0)
         nc.sync.dma_start(partner_list[:], offs2)
         load_wp(0, 0, 0)
+        load_x_scales_both()
+        nc.sync.dma_start(token_list[:], offs)
+        gather_scales(0)
         load_wp(0, 1, 8192)
-        load_x(0)
+        load_wp(1, 0, 16384)
+        load_x(1)
         load_scales(w1s, w1_scales.rearrange("e s b i -> (e s) b i"))
         load_w1(0)
-        load_wp(1, 0, 16384)
-        gather_scales(0)
+        load_gate(0, 2)
         load_wp(1, 1, 24576)
         load_w2(0)
-        load_wp(2, 0, 32768)
         load_scales(w2s, w2_scales.rearrange("e s b n -> (e s) b n"))
+        load_wp(2, 0, 32768)
         load_w1(1)
-        load_gate(0, 2)
         load_wp(2, 1, 40960)
         load_wp(3, 0, 49152)
-        load_w2(4)
-        load_w2(1)
         load_wp(3, 1, 57344)
+        load_w2(1)
         load_w1(2)
         load_wp(4, 0, 65536)
-        load_wp(4, 1, 73728)
-        load_w1(3)
         load_gate(2, 4)
+        load_w1(3)
+        load_wp(4, 1, 73728)
         load_w2(2)
-        load_w1(4)
         load_wp(5, 0, 81920)
         load_wp(5, 1, 90112)
-        load_gate(4, 6)
+        load_w1(4)
+        load_w2(4)
+        load_w2(5)
         load_w2(3)
         load_w1(5)
-        load_w2(5)
-        gather_words(0, 1, 0, 147456)
-        gather_words(1, 1, 1, 148480)
-        gather_words(0, 0, 1, 150528)
+        load_gate(4, 6)
         gather_words(0, 0, 0, 151552)
+        gather_words(0, 1, 0, 152576)
+        gather_words(1, 1, 0, 153600)
+        gather_words(0, 1, 1, 155648)
+        gather_words(0, 0, 1, 156672)
         gather_scales(1)
-        gather_words(0, 1, 1, 152576)
-        new_grouped(0, 0, 98304)
-        cast_wp(nc.scalar.copy, 0, 0, 0, 512)
+        new_grouped(0, 0, 100352)
+        cast_wp(nc.scalar.copy, 0, 0, 0, 256)
+        cast_wp(nc.scalar.copy, 0, 0, 256, 512)
         quantise_wp(0, 0, None)
-        new_grouped(0, 1, 122880)
-        cast_wp(nc.scalar.copy, 0, 1, 0, 256)
-        cast_wp(nc.scalar.copy, 0, 1, 256, 512)
+        new_grouped(0, 1, 126976)
+        cast_wp(nc.scalar.copy, 0, 1, 0, 512)
         quantise_wp(0, 1, None)
-        gather_words(1, 0, 1, 122880)
-        gather_words(1, 0, 0, 124928)
-        new_grouped(1, 0, 102400)
-        cast_wp(nc.scalar.copy, 1, 0, 0, 512)
+        gather_words(1, 1, 1, 124992)
+        gather_words(1, 0, 1, 127040)
+        gather_words(1, 0, 0, 129088)
+        new_grouped(1, 0, 104576)
+        cast_wp(nc.scalar.copy, 1, 0, 0, 256)
+        layer1(0, ((1, 0), (1, 1), (0, 0), (0, 1)))
+        activate(0, 0)
+        cast_wp(nc.scalar.copy, 1, 0, 256, 512)
         quantise_wp(1, 0, None)
-        new_grouped(1, 1, 126976)
+        new_grouped(1, 1, 131200)
         cast_wp(nc.scalar.copy, 1, 1, 0, 256)
         cast_wp(nc.vector.tensor_copy, 1, 1, 256, 512)
         quantise_wp(1, 1, None)
-        gather_words(1, 1, 0, 126976)
-        new_grouped(2, 0, 106432)
+        new_grouped(2, 0, 108608)
         cast_wp(nc.scalar.copy, 2, 0, 0, 512)
         quantise_wp(2, 0, None)
-        layer1(0, ((1, 0), (0, 0), (0, 1), (1, 1)))
-        activate(0, 0)
         layer1(1, ((1, 0), (0, 0), (0, 1), (1, 1)))
         activate(1, 16384)
-        new_grouped(2, 1, 131008)
-        cast_wp(nc.scalar.copy, 2, 1, 0, 256)
+        regroup_h(0, 1024)
+        layer2(0)
+        new_grouped(2, 1, 135232)
+        cast_wp(nc.scalar.copy, 2, 1, 0, 96)
+        drain_y(0, 0, 2, 2048)
         regroup_h(1, 17408)
         layer2(1)
-        cast_wp(nc.scalar.copy, 2, 1, 256, 512)
+        cast_wp(nc.scalar.copy, 2, 1, 96, 192)
+        cast_wp(nc.vector.tensor_copy, 2, 1, 192, 512)
         quantise_wp(2, 1, None)
-        new_grouped(3, 0, 110464)
-        cast_wp(nc.scalar.copy, 3, 0, 0, 192)
-        cast_wp(nc.vector.tensor_copy, 3, 0, 192, 512)
-        quantise_wp(3, 0, None)
-        regroup_h(0, 18432)
-        layer2(0)
-        drain_y(0, 0, 4, 19456)
-        new_grouped(3, 1, 135040)
-        cast_wp(nc.scalar.copy, 3, 1, 0, 512)
-        quantise_wp(3, 1, None)
-        layer1(2, ((1, 0), (0, 0), (0, 1), (1, 1)))
+        layer1(2, ((1, 0), (1, 1), (0, 0), (0, 1)))
         activate(2, 32768)
-        regroup_h(2, 57344)
+        new_grouped(3, 0, 112640)
+        cast_wp(nc.scalar.copy, 3, 0, 0, 384)
+        cast_wp(nc.vector.tensor_copy, 3, 0, 384, 512)
+        quantise_wp(3, 0, None)
+        new_grouped(3, 1, 139264)
+        cast_wp(nc.scalar.copy, 3, 1, 0, 448)
+        cast_wp(nc.vector.tensor_copy, 3, 1, 448, 512)
+        quantise_wp(3, 1, None)
+        regroup_h(2, 33792)
         layer2(2)
-        new_grouped(4, 0, 114496)
-        cast_wp(nc.scalar.copy, 4, 0, 0, 384)
-        cast_wp(nc.vector.tensor_copy, 4, 0, 384, 512)
+        new_grouped(4, 0, 116672)
+        cast_wp(nc.scalar.copy, 4, 0, 0, 256)
+        cast_wp(nc.scalar.copy, 4, 0, 256, 512)
         quantise_wp(4, 0, None)
-        drain_y(2, 2, 4, 33792)
-        layer1(3, ((1, 0), (1, 1), (0, 0), (0, 1)))
-        activate(3, 65536)
-        drain_y(1, 0, 2, 21504)
-        drain_y(1, 2, 4, 22528)
-        new_grouped(4, 1, 139072)
+        drain_y(1, 0, 2, 49152)
+        new_grouped(4, 1, 143296)
         cast_wp(nc.scalar.copy, 4, 1, 0, 192)
         cast_wp(nc.vector.tensor_copy, 4, 1, 192, 512)
         quantise_wp(4, 1, None)
-        regroup_h(3, 73728)
-        layer2(3)
-        new_grouped(5, 0, 118528)
+        drain_y(1, 2, 4, 50176)
+        drain_y(0, 2, 4, 3072)
+        new_grouped(5, 0, 120704)
         cast_wp(nc.scalar.copy, 5, 0, 0, 512)
         quantise_wp(5, 0, None)
-        layer1(4, ((1, 0), (0, 0), (0, 1), (1, 1)))
-        activate(4, 81920)
-        drain_y(2, 0, 2, 74752)
-        regroup_h(4, 66560)
-        layer2(4)
-        new_grouped(5, 1, 143104)
-        cast_wp(nc.scalar.copy, 5, 1, 0, 256)
-        cast_wp(nc.vector.tensor_copy, 5, 1, 256, 512)
+        layer1(3, ((0, 0), (0, 1), (1, 0), (1, 1)))
+        activate(3, 51200)
+        drain_y(2, 0, 2, 57344)
+        regroup_h(3, 52224)
+        layer2(3)
+        new_grouped(5, 1, 147328)
+        cast_wp(nc.scalar.copy, 5, 1, 0, 512)
         quantise_wp(5, 1, None)
-        layer1(5, ((0, 0), (0, 1), (1, 0), (1, 1)))
-        activate(5, 82944)
-        drain_y(3, 0, 2, 83968)
-        regroup_h(5, 84992)
+        layer1(4, ((1, 0), (0, 0), (0, 1), (1, 1)))
+        activate(4, 65536)
+        drain_y(3, 0, 4, 65536)
+        layer1(5, ((1, 0), (1, 1), (0, 0), (0, 1)))
+        activate(5, 81920)
+        drain_y(2, 2, 4, 34816)
+        regroup_h(5, 83968)
         layer2(5)
-        drain_y(4, 2, 4, 82944)
+        drain_y(5, 2, 4, 84992)
+        regroup_h(4, 67584)
+        layer2(4)
         drain_y(5, 0, 2, 86016)
-        drain_y(3, 2, 4, 81920)
-        drain_y(5, 2, 4, 87040)
-        drain_y(4, 0, 2, 90112)
+        drain_y(4, 0, 4, 81920)
         scatter(0, 0)
         scatter(0, 1)
         scatter(0, 2)
@@ -356,15 +358,15 @@ def tile_moe_duo_silu_kernel(
         scatter(3, 1)
         scatter(3, 2)
         scatter(3, 3)
-        scatter(4, 1)
+        scatter(4, 2)
         scatter(4, 0)
+        scatter(5, 0)
+        scatter(4, 1)
+        scatter(5, 2)
         scatter(5, 1)
         scatter(4, 3)
         scatter(5, 3)
-        scatter(5, 0)
-        scatter(4, 2)
-        scatter(5, 2)
-        store(1)
-        store(3)
         store(0)
         store(2)
+        store(1)
+        store(3)

@@ -70,16 +70,16 @@ def tile_moe_duo_silu_kernel(
         nc.vector.memset(zero_in[:], 0.0)
         nc.scalar.activation(out=zero_bias[:], in_=zero_in[:], func=SILU)
         nc.vector.memset(as_i32(w1s), 0)
+        nc.vector.memset(as_i32(w2s), 0)
         nc.vector.memset(token_scales_second[:].bitcast(I32), 0)
         nc.vector.memset(result[0][:], 0.0)
-        nc.gpsimd.memset(as_i32(w2s), 0)
         make_identity(nc, ident[:])
         for c in range(1, N_TILES):
-            nc.gpsimd.memset(result[c][:], 0.0)
+            nc.scalar.copy(out=result[c][:], in_=result[0][:])
 
         def load_scales(plane, rows):
             for r in range(4):
-                nc.sync.dma_start(
+                nc.gpsimd.dma_start(
                     out=plane[r:P:32, :, :].bitcast(I32),
                     in_=rows[:, r:16:4, :].rearrange("g q n -> q g n").bitcast(I32),
                 )
@@ -207,69 +207,69 @@ def tile_moe_duo_silu_kernel(
 
         def drain_y(e, first, last, offset):
             part = placed([P, last - first, C], F32, "y_sb%d_%d" % (e, first), offset)
-            weights = gate_sb[e].unsqueeze(1).to_broadcast([P, last - first, C])
-            nc.vector.tensor_tensor(part[:], y[e][:, first:last, :], weights, MULT)
+            nc.scalar.copy(out=part[:], in_=y[e][:, first:last, :])
             for c in range(first, last):
                 y_sb[(e, c)] = part[:, c - first, :]
 
         def scatter(e, c):
             cols = slice(e * C // LIST_COL, (e + 1) * C // LIST_COL)
-            nc.vector.tensor_copy(out=result[c][:].indirect(token_list[:, cols]), in_=y_sb[(e, c)])
+            nc.vector.tensor_tensor(result[c][:].indirect(token_list[:, cols]), y_sb[(e, c)], gate_sb[e], MULT)
 
         def store(c):
             nc.sync.dma_start(out=out[c * P : (c + 1) * P, :], in_=result[c][:])
 
-        load_x(0)
+        load_scales(w1s, w1_scales.rearrange("e s b i -> (e s) b i"))
+        load_scales(w2s, w2_scales.rearrange("e s b n -> (e s) b n"))
         nc.sync.dma_start(partner_list[:], offs2)
-        load_wp(0, 0, 0)
-        load_x_scales_both()
         nc.sync.dma_start(token_list[:], offs)
-        gather_scales(0)
+        load_x(0)
+        load_x_scales_both()
+        load_wp(0, 0, 0)
         load_wp(0, 1, 8192)
         load_wp(1, 0, 16384)
         load_x(1)
-        load_scales(w1s, w1_scales.rearrange("e s b i -> (e s) b i"))
+        load_w1(1)
+        load_wp(1, 1, 24576)
+        gather_scales(0)
         load_w1(0)
         load_gate(0, 2)
-        load_wp(1, 1, 24576)
-        load_w2(0)
-        load_scales(w2s, w2_scales.rearrange("e s b n -> (e s) b n"))
+        load_w1(2)
         load_wp(2, 0, 32768)
-        load_w1(1)
         load_wp(2, 1, 40960)
+        load_w2(0)
         load_wp(3, 0, 49152)
         load_wp(3, 1, 57344)
         load_w2(1)
-        load_w1(2)
-        load_wp(4, 0, 65536)
-        load_gate(2, 4)
         load_w1(3)
+        load_wp(4, 0, 65536)
         load_wp(4, 1, 73728)
         load_w2(2)
         load_wp(5, 0, 81920)
-        load_wp(5, 1, 90112)
+        load_gate(2, 4)
         load_w1(4)
-        load_w2(4)
-        load_w2(5)
         load_w2(3)
+        load_wp(5, 1, 90112)
+        load_w2(4)
         load_w1(5)
         load_gate(4, 6)
-        gather_words(0, 0, 0, 151552)
-        gather_words(0, 1, 0, 152576)
-        gather_words(1, 1, 0, 153600)
-        gather_words(0, 1, 1, 155648)
-        gather_words(0, 0, 1, 156672)
+        load_w2(5)
+        gather_words(0, 1, 0, 151552)
+        gather_words(0, 0, 1, 152576)
         gather_scales(1)
+        gather_words(0, 1, 1, 153600)
+        gather_words(0, 0, 0, 154624)
         new_grouped(0, 0, 100352)
         cast_wp(nc.scalar.copy, 0, 0, 0, 256)
-        cast_wp(nc.scalar.copy, 0, 0, 256, 512)
+        cast_wp(nc.vector.tensor_copy, 0, 0, 256, 512)
         quantise_wp(0, 0, None)
         new_grouped(0, 1, 126976)
-        cast_wp(nc.scalar.copy, 0, 1, 0, 512)
+        cast_wp(nc.scalar.copy, 0, 1, 0, 96)
+        cast_wp(nc.scalar.copy, 0, 1, 96, 192)
+        cast_wp(nc.vector.tensor_copy, 0, 1, 192, 512)
         quantise_wp(0, 1, None)
-        gather_words(1, 1, 1, 124992)
-        gather_words(1, 0, 1, 127040)
-        gather_words(1, 0, 0, 129088)
+        gather_words(1, 0, 1, 124992)
+        gather_words(1, 0, 0, 127040)
+        gather_words(1, 1, 1, 129088)
         new_grouped(1, 0, 104576)
         cast_wp(nc.scalar.copy, 1, 0, 0, 256)
         layer1(0, ((1, 0), (1, 1), (0, 0), (0, 1)))
@@ -277,71 +277,74 @@ def tile_moe_duo_silu_kernel(
         cast_wp(nc.scalar.copy, 1, 0, 256, 512)
         quantise_wp(1, 0, None)
         new_grouped(1, 1, 131200)
-        cast_wp(nc.scalar.copy, 1, 1, 0, 256)
-        cast_wp(nc.vector.tensor_copy, 1, 1, 256, 512)
+        cast_wp(nc.scalar.copy, 1, 1, 0, 160)
+        cast_wp(nc.scalar.copy, 1, 1, 160, 320)
+        cast_wp(nc.vector.tensor_copy, 1, 1, 320, 512)
         quantise_wp(1, 1, None)
+        gather_words(1, 1, 0, 131200)
         new_grouped(2, 0, 108608)
-        cast_wp(nc.scalar.copy, 2, 0, 0, 512)
+        cast_wp(nc.scalar.copy, 2, 0, 0, 160)
+        cast_wp(nc.scalar.copy, 2, 0, 160, 320)
+        cast_wp(nc.vector.tensor_copy, 2, 0, 320, 512)
         quantise_wp(2, 0, None)
-        layer1(1, ((1, 0), (0, 0), (0, 1), (1, 1)))
-        activate(1, 16384)
-        regroup_h(0, 1024)
-        layer2(0)
+        layer1(1, ((1, 0), (1, 1), (0, 0), (0, 1)))
+        activate(1, 32768)
         new_grouped(2, 1, 135232)
-        cast_wp(nc.scalar.copy, 2, 1, 0, 96)
-        drain_y(0, 0, 2, 2048)
-        regroup_h(1, 17408)
-        layer2(1)
-        cast_wp(nc.scalar.copy, 2, 1, 96, 192)
+        cast_wp(nc.scalar.copy, 2, 1, 0, 192)
         cast_wp(nc.vector.tensor_copy, 2, 1, 192, 512)
         quantise_wp(2, 1, None)
-        layer1(2, ((1, 0), (1, 1), (0, 0), (0, 1)))
-        activate(2, 32768)
+        regroup_h(1, 16384)
+        layer2(1)
+        regroup_h(0, 17408)
+        layer2(0)
+        layer1(2, ((0, 0), (0, 1), (1, 0), (1, 1)))
+        activate(2, 33792)
         new_grouped(3, 0, 112640)
-        cast_wp(nc.scalar.copy, 3, 0, 0, 384)
-        cast_wp(nc.vector.tensor_copy, 3, 0, 384, 512)
+        cast_wp(nc.scalar.copy, 3, 0, 0, 224)
+        cast_wp(nc.scalar.copy, 3, 0, 224, 448)
+        cast_wp(nc.vector.tensor_copy, 3, 0, 448, 512)
         quantise_wp(3, 0, None)
+        drain_y(0, 0, 2, 34816)
         new_grouped(3, 1, 139264)
-        cast_wp(nc.scalar.copy, 3, 1, 0, 448)
-        cast_wp(nc.vector.tensor_copy, 3, 1, 448, 512)
+        cast_wp(nc.scalar.copy, 3, 1, 0, 320)
+        cast_wp(nc.vector.tensor_copy, 3, 1, 320, 512)
         quantise_wp(3, 1, None)
-        regroup_h(2, 33792)
+        drain_y(0, 2, 4, 1024)
+        drain_y(1, 0, 4, 35840)
+        regroup_h(2, 37888)
         layer2(2)
+        layer1(3, ((0, 0), (0, 1), (1, 1), (1, 0)))
+        activate(3, 49152)
         new_grouped(4, 0, 116672)
-        cast_wp(nc.scalar.copy, 4, 0, 0, 256)
-        cast_wp(nc.scalar.copy, 4, 0, 256, 512)
+        cast_wp(nc.scalar.copy, 4, 0, 0, 512)
         quantise_wp(4, 0, None)
-        drain_y(1, 0, 2, 49152)
+        regroup_h(3, 50176)
+        layer2(3)
         new_grouped(4, 1, 143296)
-        cast_wp(nc.scalar.copy, 4, 1, 0, 192)
-        cast_wp(nc.vector.tensor_copy, 4, 1, 192, 512)
+        cast_wp(nc.scalar.copy, 4, 1, 0, 512)
         quantise_wp(4, 1, None)
-        drain_y(1, 2, 4, 50176)
-        drain_y(0, 2, 4, 3072)
+        drain_y(2, 0, 4, 38912)
+        layer1(4, ((1, 0), (0, 0), (0, 1), (1, 1)))
+        activate(4, 65536)
         new_grouped(5, 0, 120704)
         cast_wp(nc.scalar.copy, 5, 0, 0, 512)
         quantise_wp(5, 0, None)
-        layer1(3, ((0, 0), (0, 1), (1, 0), (1, 1)))
-        activate(3, 51200)
-        drain_y(2, 0, 2, 57344)
-        regroup_h(3, 52224)
-        layer2(3)
+        drain_y(3, 2, 4, 51200)
         new_grouped(5, 1, 147328)
-        cast_wp(nc.scalar.copy, 5, 1, 0, 512)
-        quantise_wp(5, 1, None)
-        layer1(4, ((1, 0), (0, 0), (0, 1), (1, 1)))
-        activate(4, 65536)
-        drain_y(3, 0, 4, 65536)
-        layer1(5, ((1, 0), (1, 1), (0, 0), (0, 1)))
-        activate(5, 81920)
-        drain_y(2, 2, 4, 34816)
-        regroup_h(5, 83968)
-        layer2(5)
-        drain_y(5, 2, 4, 84992)
-        regroup_h(4, 67584)
+        cast_wp(nc.scalar.copy, 5, 1, 0, 256)
+        regroup_h(4, 66560)
         layer2(4)
-        drain_y(5, 0, 2, 86016)
-        drain_y(4, 0, 4, 81920)
+        cast_wp(nc.scalar.copy, 5, 1, 256, 512)
+        quantise_wp(5, 1, None)
+        drain_y(3, 0, 2, 65536)
+        drain_y(4, 2, 4, 67584)
+        layer1(5, ((1, 0), (0, 0), (0, 1), (1, 1)))
+        activate(5, 81920)
+        regroup_h(5, 82944)
+        layer2(5)
+        drain_y(4, 0, 2, 81920)
+        drain_y(5, 0, 2, 83968)
+        drain_y(5, 2, 4, 84992)
         scatter(0, 0)
         scatter(0, 1)
         scatter(0, 2)
@@ -358,13 +361,13 @@ def tile_moe_duo_silu_kernel(
         scatter(3, 1)
         scatter(3, 2)
         scatter(3, 3)
-        scatter(4, 2)
         scatter(4, 0)
-        scatter(5, 0)
+        scatter(4, 3)
         scatter(4, 1)
+        scatter(4, 2)
+        scatter(5, 0)
         scatter(5, 2)
         scatter(5, 1)
-        scatter(4, 3)
         scatter(5, 3)
         store(0)
         store(2)

from contextlib import ExitStack

import concourse.mybir as mybir
from concourse.masks import make_identity

K, T, E, C, H, N = 1024, 1024, 6, 128, 512, 512
FLOPS = 2 * E * C * (2 * K * H + H * N)

F32 = mybir.dt.float32
BF16 = mybir.dt.bfloat16
I32 = mybir.dt.int32
U32 = mybir.dt.uint32
U16 = mybir.dt.uint16
U8 = mybir.dt.uint8
FP8X4 = mybir.dt.float8_e4m3fn_x4
FP4X4 = mybir.dt.float4_e2m1fn_x4
SILU = mybir.ActivationFunctionType.Silu
MULT = mybir.AluOpType.mult

P = 128
PACK = 4
K_PASS = P * PACK
PASSES = K // K_PASS
SLOTS = E * C
LIST_COL = 16
GROUPS = ((0, 2), (2, 6))
N_TILES = N // P
HALF = H // 2


def tile_moe_duo_silu_kernel(
    tc, x_words, x_scales, w1_words, w1_scales, wp, w2_words, w2_scales, gate, offs, offs2, out
):
    nc = tc.nc
    with ExitStack() as ctx:
        lists = ctx.enter_context(tc.tile_pool(name="lists", bufs=1))
        keep = ctx.enter_context(tc.tile_pool(name="keep", bufs=1))
        ring = ctx.enter_context(tc.tile_pool(name="ring", bufs=3))
        arena = ctx.enter_context(tc.tile_pool(name="arena", bufs=1))
        psum = ctx.enter_context(tc.psum_pool(name="psum", bufs=2))

        def placed(shape, dtype, name, offset):
            return arena.tile(shape, dtype, name=name, align_bytes=64, offset=offset)

        def held(shape, dtype, name):
            return keep.tile(shape, dtype, name=name, align_bytes=64)

        token_list = lists.tile([P, SLOTS // LIST_COL], U16, name="token_list")
        partner_list = lists.tile([P, SLOTS // LIST_COL], U16, name="partner_list")
        index_lists = (token_list, partner_list)

        xw = [held([P, T], U32, "xw%d" % s) for s in range(PASSES)]
        xs = held([P, T], U8, "xs")
        token_scales_second = held([P, SLOTS], U8, "token_scales_second")
        w1s = held([P, E * PASSES, H], U8, "w1s")
        w2s = held([P, E, N], U8, "w2s")
        w1w = [held([P, PASSES, 2 * H], U8, "w1w%d" % e) for e in range(E)]
        w2w = [held([P, 2 * N], U8, "w2w%d" % e) for e in range(E)]
        wp_raw = {}
        gate_sb = {}
        result = [held([P, T], F32, "result%d" % c) for c in range(N_TILES)]
        ident = held([P, P], F32, "ident")
        zero_in = held([P, 1], F32, "zero_in")
        zero_bias = held([P, 1], F32, "zero_bias")

        def as_i32(plane):
            return plane[:].rearrange("p a b -> p (a b)").bitcast(I32)

        nc.vector.memset(xs[:].bitcast(I32), 0)
        nc.vector.memset(zero_in[:], 0.0)
        nc.scalar.activation(out=zero_bias[:], in_=zero_in[:], func=SILU)
        nc.vector.memset(as_i32(w1s), 0)
        nc.vector.memset(as_i32(w2s), 0)
        nc.vector.memset(token_scales_second[:].bitcast(I32), 0)
        nc.vector.memset(result[0][:], 0.0)
        make_identity(nc, ident[:])
        for c in range(1, N_TILES):
            nc.scalar.copy(out=result[c][:], in_=result[0][:])

        def load_scales(plane, rows):
            for r in range(4):
                nc.gpsimd.dma_start(
                    out=plane[r:P:32, :, :].bitcast(I32),
                    in_=rows[:, r:16:4, :].rearrange("g q n -> q g n").bitcast(I32),
                )

        def load_x(s):
            nc.sync.dma_start(out=xw[s][:].bitcast(I32), in_=x_words[s].rearrange("p t d -> p (t d)").bitcast(I32))

        def load_wp(e, s, offset):
            wp_raw[(e, s)] = placed([P, PACK, H], F32, "wp_raw%d_%d" % (e, s), offset)
            rows = wp[e, s * K_PASS : (s + 1) * K_PASS, :].rearrange("(p j) i -> p j i", j=PACK)
            nc.sync.dma_start(out=wp_raw[(e, s)][:], in_=rows)

        def load_x_scales_both():
            for q in range(4):
                nc.sync.dma_start(
                    out=xs[32 * q : 32 * q + 8, :].bitcast(I32), in_=x_scales[:, 4 * q : 4 * q + 4, :].bitcast(I32)
                )

        def load_gate(first, last):
            part = held([P, (last - first) * C], F32, "gate%d" % first)
            nc.sync.dma_start(out=part[:], in_=gate[:, first * C : last * C])
            for e in range(first, last):
                gate_sb[e] = part[:, (e - first) * C : (e - first + 1) * C]

        def load_w1(e):
            nc.sync.dma_start(out=w1w[e][:].bitcast(I32), in_=w1_words[e].rearrange("s p b -> p s b").bitcast(I32))

        def load_w2(e):
            nc.sync.dma_start(out=w2w[e][:].bitcast(I32), in_=w2_words[e, 0].bitcast(I32))

        gathered_words = {}
        gathered_scales = {}

        def gather_words(group, which, s, offset):
            first, last = GROUPS[group]
            words = placed([P, (last - first) * C], U32, "gw%d_%d_%d" % (group, which, s), offset)
            cols = slice(first * C // LIST_COL, last * C // LIST_COL)
            nc.vector.tensor_copy(out=words[:], in_=xw[s][:].indirect(index_lists[which][:, cols]))
            for e in range(first, last):
                gathered_words[(e, which, s)] = words[:, (e - first) * C : (e - first + 1) * C]

        def gather_scales(which):
            scales = held([P, SLOTS], U8, "gs%d" % which)
            nc.vector.tensor_copy(out=scales[:], in_=xs[:].indirect(index_lists[which][:]))
            gathered_scales[which] = scales
            if which == 0:
                for r in range(4):
                    nc.sync.dma_start(
                        out=token_scales_second[r:P:32, :].bitcast(I32), in_=scales[r + 4 : P : 32, :].bitcast(I32)
                    )

        grouped = {}
        wp_q = {}

        def new_grouped(e, s, offset):
            grouped[(e, s)] = placed([P, PACK * H], BF16, "grouped%d_%d" % (e, s), offset)

        def cast_wp(copy, e, s, first, last):
            copy(
                out=grouped[(e, s)][:, PACK * first : PACK * last].rearrange("p (c i t) -> p c t i", i=4, t=PACK),
                in_=wp_raw[(e, s)][:, :, first:last].rearrange("p t (c i) -> p c t i", i=4),
            )

        def quantise_wp(e, s, offset):
            if offset is None:
                codes = ring.tile([P, H], U32, name="wp_codes", align_bytes=64, bufs=4)
            else:
                codes = placed([P, H], U32, "wp_codes%d_%d" % (e, s), offset)
            scales = ring.tile([P, H], U8, name="wp_scales", align_bytes=64, bufs=4)
            nc.vector.quantize_mx(out=codes[:].bitcast(FP8X4), scales=scales[:], in_=grouped[(e, s)][:])
            wp_q[(e, s)] = (codes[:].bitcast(FP8X4), scales[:])

        pre = {}
        turned = {}
        h_grouped = {}
        y = {}
        y_sb = {}

        def layer1(e, order):
            cols = slice(e * C, (e + 1) * C)
            token_scales = (gathered_scales[0], token_scales_second)
            pre[e] = psum.tile([P, H], F32, name="pre", bufs=1)
            for place, (which, s) in enumerate(order):
                if which == 0:
                    slot_scales = token_scales[s][:, cols]
                    codes, code_scales = w1w[e][:, s, :].bitcast(FP4X4), w1s[:, e * PASSES + s, :]
                else:
                    slot_scales = gathered_scales[1][4 * s : P, cols]
                    codes, code_scales = wp_q[(e, s)]
                nc.tensor.matmul_mx(
                    out=pre[e][:], lhsT=gathered_words[(e, which, s)].bitcast(FP8X4), lhsT_scale=slot_scales,
                    rhs=codes, rhs_scale=code_scales, start=(place == 0), stop=(place == len(order) - 1),
                )

        def activate(e, offset):
            h = placed([P, H], BF16, "h%d" % e, offset)
            nc.scalar.activation(
                out=h[:].rearrange("c (u p d) -> c u p d", u=2, d=2),
                in_=pre[e][:].rearrange("c (p u d) -> c u p d", u=2, d=2),
                func=SILU, bias=zero_bias[:],
            )
            h_words = h[:].bitcast(F32)
            turned[e] = psum.tile([P, 2, C], F32, name="turned")
            for u in range(2):
                nc.tensor.transpose(turned[e][:, u, :], h_words[:, u * P : (u + 1) * P], ident[:])

        def regroup_h(e, offset):
            h_grouped[e] = placed([P, PACK * C], BF16, "h_grouped%d" % e, offset)
            nc.scalar.copy(
                out=h_grouped[e][:].bitcast(F32).rearrange("p (c u) -> p c u", u=2),
                in_=turned[e][:].rearrange("p u c -> p c u"),
            )

        def layer2(e):
            codes = ring.tile([P, C], U32, name="h_codes", align_bytes=64)
            scales = ring.tile([P, C], U8, name="h_scales", align_bytes=64)
            nc.vector.quantize_mx(out=codes[:].bitcast(FP8X4), scales=scales[:], in_=h_grouped[e][:])
            y[e] = psum.tile([P, N_TILES, C], F32, name="y", bufs=3)
            for c in range(N_TILES):
                nc.tensor.matmul_mx(
                    out=y[e][:, c, :], lhsT=w2w[e][:, 2 * P * c : 2 * P * (c + 1)].bitcast(FP4X4),
                    lhsT_scale=w2s[:, e, P * c : P * (c + 1)],
                    rhs=codes[:].bitcast(FP8X4), rhs_scale=scales[:], start=True, stop=True,
                )

        def drain_y(e, first, last, offset):
            part = placed([P, last - first, C], F32, "y_sb%d_%d" % (e, first), offset)
            nc.scalar.copy(out=part[:], in_=y[e][:, first:last, :])
            for c in range(first, last):
                y_sb[(e, c)] = part[:, c - first, :]

        def scatter(e, c):
            cols = slice(e * C // LIST_COL, (e + 1) * C // LIST_COL)
            nc.vector.tensor_tensor(result[c][:].indirect(token_list[:, cols]), y_sb[(e, c)], gate_sb[e], MULT)

        def store(c):
            nc.sync.dma_start(out=out[c * P : (c + 1) * P, :], in_=result[c][:])

        load_scales(w1s, w1_scales.rearrange("e s b i -> (e s) b i"))
        load_scales(w2s, w2_scales.rearrange("e s b n -> (e s) b n"))
        nc.sync.dma_start(partner_list[:], offs2)
        nc.sync.dma_start(token_list[:], offs)
        load_x(0)
        load_x_scales_both()
        load_wp(0, 0, 0)
        load_wp(0, 1, 8192)
        load_wp(1, 0, 16384)
        load_x(1)
        load_w1(1)
        load_wp(1, 1, 24576)
        gather_scales(0)
        load_w1(0)
        load_gate(0, 2)
        load_w1(2)
        load_wp(2, 0, 32768)
        load_wp(2, 1, 40960)
        load_w2(0)
        load_wp(3, 0, 49152)
        load_wp(3, 1, 57344)
        load_w2(1)
        load_w1(3)
        load_wp(4, 0, 65536)
        load_wp(4, 1, 73728)
        load_w2(2)
        load_wp(5, 0, 81920)
        load_gate(2, 4)
        load_w1(4)
        load_w2(3)
        load_wp(5, 1, 90112)
        load_w2(4)
        load_w1(5)
        load_gate(4, 6)
        load_w2(5)
        gather_words(0, 1, 0, 151552)
        gather_words(0, 0, 1, 152576)
        gather_scales(1)
        gather_words(0, 1, 1, 153600)
        gather_words(0, 0, 0, 154624)
        new_grouped(0, 0, 100352)
        cast_wp(nc.scalar.copy, 0, 0, 0, 256)
        cast_wp(nc.vector.tensor_copy, 0, 0, 256, 512)
        quantise_wp(0, 0, None)
        new_grouped(0, 1, 126976)
        cast_wp(nc.scalar.copy, 0, 1, 0, 96)
        cast_wp(nc.scalar.copy, 0, 1, 96, 192)
        cast_wp(nc.vector.tensor_copy, 0, 1, 192, 512)
        quantise_wp(0, 1, None)
        gather_words(1, 0, 1, 124992)
        gather_words(1, 0, 0, 127040)
        gather_words(1, 1, 1, 129088)
        new_grouped(1, 0, 104576)
        cast_wp(nc.scalar.copy, 1, 0, 0, 256)
        layer1(0, ((1, 0), (1, 1), (0, 0), (0, 1)))
        activate(0, 0)
        cast_wp(nc.scalar.copy, 1, 0, 256, 512)
        quantise_wp(1, 0, None)
        new_grouped(1, 1, 131200)
        cast_wp(nc.scalar.copy, 1, 1, 0, 160)
        cast_wp(nc.scalar.copy, 1, 1, 160, 320)
        cast_wp(nc.vector.tensor_copy, 1, 1, 320, 512)
        quantise_wp(1, 1, None)
        gather_words(1, 1, 0, 131200)
        new_grouped(2, 0, 108608)
        cast_wp(nc.scalar.copy, 2, 0, 0, 160)
        cast_wp(nc.scalar.copy, 2, 0, 160, 320)
        cast_wp(nc.vector.tensor_copy, 2, 0, 320, 512)
        quantise_wp(2, 0, None)
        layer1(1, ((1, 0), (1, 1), (0, 0), (0, 1)))
        activate(1, 32768)
        new_grouped(2, 1, 135232)
        cast_wp(nc.scalar.copy, 2, 1, 0, 192)
        cast_wp(nc.vector.tensor_copy, 2, 1, 192, 512)
        quantise_wp(2, 1, None)
        regroup_h(1, 16384)
        layer2(1)
        regroup_h(0, 17408)
        layer2(0)
        layer1(2, ((0, 0), (0, 1), (1, 0), (1, 1)))
        activate(2, 33792)
        new_grouped(3, 0, 112640)
        cast_wp(nc.scalar.copy, 3, 0, 0, 224)
        cast_wp(nc.scalar.copy, 3, 0, 224, 448)
        cast_wp(nc.vector.tensor_copy, 3, 0, 448, 512)
        quantise_wp(3, 0, None)
        drain_y(0, 0, 2, 34816)
        new_grouped(3, 1, 139264)
        cast_wp(nc.scalar.copy, 3, 1, 0, 320)
        cast_wp(nc.vector.tensor_copy, 3, 1, 320, 512)
        quantise_wp(3, 1, None)
        drain_y(0, 2, 4, 1024)
        drain_y(1, 0, 4, 35840)
        regroup_h(2, 37888)
        layer2(2)
        layer1(3, ((0, 0), (0, 1), (1, 1), (1, 0)))
        activate(3, 49152)
        new_grouped(4, 0, 116672)
        cast_wp(nc.scalar.copy, 4, 0, 0, 512)
        quantise_wp(4, 0, None)
        regroup_h(3, 50176)
        layer2(3)
        new_grouped(4, 1, 143296)
        cast_wp(nc.scalar.copy, 4, 1, 0, 512)
        quantise_wp(4, 1, None)
        drain_y(2, 0, 4, 38912)
        layer1(4, ((1, 0), (0, 0), (0, 1), (1, 1)))
        activate(4, 65536)
        new_grouped(5, 0, 120704)
        cast_wp(nc.scalar.copy, 5, 0, 0, 512)
        quantise_wp(5, 0, None)
        drain_y(3, 2, 4, 51200)
        new_grouped(5, 1, 147328)
        cast_wp(nc.scalar.copy, 5, 1, 0, 256)
        regroup_h(4, 66560)
        layer2(4)
        cast_wp(nc.scalar.copy, 5, 1, 256, 512)
        quantise_wp(5, 1, None)
        drain_y(3, 0, 2, 65536)
        drain_y(4, 2, 4, 67584)
        layer1(5, ((1, 0), (0, 0), (0, 1), (1, 1)))
        activate(5, 81920)
        regroup_h(5, 82944)
        layer2(5)
        drain_y(4, 0, 2, 81920)
        drain_y(5, 0, 2, 83968)
        drain_y(5, 2, 4, 84992)
        scatter(0, 0)
        scatter(0, 1)
        scatter(0, 2)
        scatter(0, 3)
        scatter(1, 0)
        scatter(1, 1)
        scatter(1, 2)
        scatter(1, 3)
        scatter(2, 0)
        scatter(2, 1)
        scatter(2, 2)
        scatter(2, 3)
        scatter(3, 0)
        scatter(3, 1)
        scatter(3, 2)
        scatter(3, 3)
        scatter(4, 0)
        scatter(4, 3)
        scatter(4, 1)
        scatter(4, 2)
        scatter(5, 0)
        scatter(5, 2)
        scatter(5, 1)
        scatter(5, 3)
        store(0)
        store(2)
        store(1)
        store(3)
